import numpy as np
import ml_dtypes

BF16 = ml_dtypes.bfloat16


def bf(x):
    return np.asarray(x, np.float32).astype(BF16)


def f32(x):
    return np.asarray(x, np.float32)


def f64(x):
    return np.asarray(x).astype(np.float64)


def striped(idx):
    return np.tile(idx.reshape(-1, 16).T, (8, 1))


S, K, M, N, T, D = 512, 128, 384, 128, 128, 128


def setup_inputs():
    return {"base": bf(np.random.standard_normal((M, S))), "q": bf(1.5 * np.random.standard_normal((K, N)) / np.sqrt(K)), "k": bf(np.random.standard_normal((K, T))), "v": bf(np.random.standard_normal((T, D))), "w": bf(2.0 * np.random.standard_normal((D, M)) / np.sqrt(D)), "offs": striped(np.random.permutation(S)[:N])}


def reference(base, q, k, v, w, offs):
    idx = offs[:16].T.reshape(-1)
    a = f64(q).T @ f64(k)
    a = np.exp(a - a.max(axis=1, keepdims=True))
    a = a / a.sum(axis=1, keepdims=True)
    z = f64(base).copy()
    z[:, idx] += f64(w).T @ (a @ f64(v)).T
    return z

@@ -1,0 +1,77 @@
+import concourse.mybir as mybir
+from concourse.masks import make_identity
+
+P = 128
+S = 512
+M = 384
+BLOCKS = M // P
+
+FLOPS = 2 * (P * P * P + P * P * P + P * M * P)
+
+BF16, F32, U16 = mybir.dt.bfloat16, mybir.dt.float32, mybir.dt.uint16
+EXP = mybir.ActivationFunctionType.Exp
+X = mybir.AxisListType.X
+
+
+def tile_rows_attnback_kernel(tc, base, q, k, v, w, offs, out):
+    nc = tc.nc
+    with (
+        tc.tile_pool(name="held", bufs=1) as held,
+        tc.psum_pool(name="psum", bufs=1) as psum,
+    ):
+        q_in = held.tile([P, P], BF16)
+        k_in = held.tile([P, P], BF16)
+        base_in = held.tile([P, BLOCKS, S], BF16)
+        v_in = held.tile([P, P], BF16)
+        w_in = held.tile([P, M], BF16)
+        offsets = held.tile([P, P // 16], U16)
+        nc.sync.dma_start(q_in[:], q)
+        nc.sync.dma_start(k_in[:], k)
+        nc.sync.dma_start(base_in[:], base.rearrange("(a p) s -> p a s", p=P))
+        nc.sync.dma_start(v_in[:], v)
+        nc.sync.dma_start(w_in[:], w)
+        nc.sync.dma_start(offsets[:], offs)
+
+        ident = held.tile([P, P], BF16)
+        make_identity(nc, ident[:])
+
+        a = psum.tile([P, P], F32)
+        nc.tensor.matmul(a[:], q_in[:], k_in[:], start=True, stop=True)
+
+        windows = [psum.tile([P, S], F32, name=f"window{m}") for m in range(BLOCKS)]
+        for m in range(BLOCKS):
+            nc.tensor.matmul(windows[m][:], ident[:], base_in[:, m, :], start=True, stop=False)
+
+        neg_max = held.tile([P, 1], F32)
+        e = held.tile([P, P], F32)
+        e_sum = held.tile([P, 1], F32)
+        inv_sum = held.tile([P, 1], F32)
+        p = held.tile([P, P], BF16)
+        nc.vector.reduce_max(neg_max[:], a[:], axis=X, negate=True)
+        nc.scalar.activation(e[:], a[:], EXP, bias=neg_max[:], accum_out=e_sum[:])
+        nc.vector.reciprocal(inv_sum[:], e_sum[:])
+        nc.vector.tensor_scalar_mul(p[:], e[:], inv_sum[:])
+
+        p_t_psum = psum.tile([P, P], BF16)
+        p_t = held.tile([P, P], BF16)
+        nc.tensor.transpose(p_t_psum[:], p[:], ident[:])
+        nc.vector.tensor_copy(p_t[:], p_t_psum[:])
+
+        o_t_psum = psum.tile([P, P], F32)
+        o_t = held.tile([P, P], BF16)
+        nc.tensor.matmul(o_t_psum[:], v_in[:], p_t[:], start=True, stop=True)
+        nc.vector.tensor_copy(o_t[:], o_t_psum[:])
+
+        for m in range(BLOCKS):
+            nc.tensor.matmul(
+                windows[m][:].indirect(offsets[:]), w_in[:, m * P : (m + 1) * P], o_t[:],
+                start=False, stop=True,
+            )
+
+        for m in range(BLOCKS):
+            z = held.tile([P, S], F32, name=f"z{m}")
+            if m % 2 == 0:
+                nc.vector.tensor_copy(z[:], windows[m][:])
+            else:
+                nc.scalar.copy(z[:], windows[m][:])
+            nc.sync.dma_start(out[m * P : (m + 1) * P, :], z[:])

@@ -6,6 +6,8 @@ S = 512
 M = 384
 BLOCKS = M // P
 
+WARM_UP = 3
+
 FLOPS = 2 * (P * P * P + P * P * P + P * M * P)
 
 BF16, F32, U16 = mybir.dt.bfloat16, mybir.dt.float32, mybir.dt.uint16
@@ -32,6 +34,12 @@ def tile_rows_attnback_kernel(tc, base, q, k, v, w, offs, out):
         nc.sync.dma_start(w_in[:], w)
         nc.sync.dma_start(offsets[:], offs)
 
+        zeros = held.tile([P, P], BF16)
+        nc.gpsimd.memset(zeros[:], 0.0)
+        spare = psum.tile([P, S], F32)
+        for _ in range(WARM_UP):
+            nc.tensor.matmul(spare[:], zeros[:], zeros[:, 0:1].to_broadcast([P, S]), start=True, stop=True)
+
         ident = held.tile([P, P], BF16)
         make_identity(nc, ident[:])
 
@@ -39,8 +47,11 @@ def tile_rows_attnback_kernel(tc, base, q, k, v, w, offs, out):
         nc.tensor.matmul(a[:], q_in[:], k_in[:], start=True, stop=True)
 
         windows = [psum.tile([P, S], F32, name=f"window{m}") for m in range(BLOCKS)]
-        for m in range(BLOCKS):
+
+        def fill(m):
             nc.tensor.matmul(windows[m][:], ident[:], base_in[:, m, :], start=True, stop=False)
+
+        fill(0)
 
         neg_max = held.tile([P, 1], F32)
         e = held.tile([P, P], F32)
@@ -55,11 +66,13 @@ def tile_rows_attnback_kernel(tc, base, q, k, v, w, offs, out):
         p_t_psum = psum.tile([P, P], BF16)
         p_t = held.tile([P, P], BF16)
         nc.tensor.transpose(p_t_psum[:], p[:], ident[:])
+        fill(1)
         nc.vector.tensor_copy(p_t[:], p_t_psum[:])
 
         o_t_psum = psum.tile([P, P], F32)
         o_t = held.tile([P, P], BF16)
         nc.tensor.matmul(o_t_psum[:], v_in[:], p_t[:], start=True, stop=True)
+        fill(2)
         nc.vector.tensor_copy(o_t[:], o_t_psum[:])
 
         for m in range(BLOCKS):

@@ -82,9 +82,10 @@ def tile_rows_attnback_kernel(tc, base, q, k, v, w, offs, out):
             )
 
         for m in range(BLOCKS):
-            z = held.tile([P, S], F32, name=f"z{m}")
-            if m % 2 == 0:
-                nc.vector.tensor_copy(z[:], windows[m][:])
-            else:
-                nc.scalar.copy(z[:], windows[m][:])
-            nc.sync.dma_start(out[m * P : (m + 1) * P, :], z[:])
+            for half in (slice(0, S // 2), slice(S // 2, S)):
+                z = held.tile([P, S // 2], F32, name=f"z{m}_{half.start}")
+                if m % 2 == 0:
+                    nc.vector.tensor_copy(z[:], windows[m][:, half])
+                else:
+                    nc.scalar.copy(z[:], windows[m][:, half])
+                nc.sync.dma_start(out[m * P : (m + 1) * P, half], z[:])

import concourse.mybir as mybir
from concourse.masks import make_identity

P = 128
S = 512
M = 384
BLOCKS = M // P

WARM_UP = 3

FLOPS = 2 * (P * P * P + P * P * P + P * M * P)

BF16, F32, U16 = mybir.dt.bfloat16, mybir.dt.float32, mybir.dt.uint16
EXP = mybir.ActivationFunctionType.Exp
X = mybir.AxisListType.X


def tile_rows_attnback_kernel(tc, base, q, k, v, w, offs, out):
    nc = tc.nc
    with (
        tc.tile_pool(name="held", bufs=1) as held,
        tc.psum_pool(name="psum", bufs=1) as psum,
    ):
        q_in = held.tile([P, P], BF16)
        k_in = held.tile([P, P], BF16)
        base_in = held.tile([P, BLOCKS, S], BF16)
        v_in = held.tile([P, P], BF16)
        w_in = held.tile([P, M], BF16)
        offsets = held.tile([P, P // 16], U16)
        nc.sync.dma_start(q_in[:], q)
        nc.sync.dma_start(k_in[:], k)
        nc.sync.dma_start(base_in[:], base.rearrange("(a p) s -> p a s", p=P))
        nc.sync.dma_start(v_in[:], v)
        nc.sync.dma_start(w_in[:], w)
        nc.sync.dma_start(offsets[:], offs)

        zeros = held.tile([P, P], BF16)
        nc.gpsimd.memset(zeros[:], 0.0)
        spare = psum.tile([P, S], F32)
        for _ in range(WARM_UP):
            nc.tensor.matmul(spare[:], zeros[:], zeros[:, 0:1].to_broadcast([P, S]), start=True, stop=True)

        ident = held.tile([P, P], BF16)
        make_identity(nc, ident[:])

        a = psum.tile([P, P], F32)
        nc.tensor.matmul(a[:], q_in[:], k_in[:], start=True, stop=True)

        windows = [psum.tile([P, S], F32, name=f"window{m}") for m in range(BLOCKS)]

        def fill(m):
            nc.tensor.matmul(windows[m][:], ident[:], base_in[:, m, :], start=True, stop=False)

        fill(0)

        neg_max = held.tile([P, 1], F32)
        e = held.tile([P, P], F32)
        e_sum = held.tile([P, 1], F32)
        inv_sum = held.tile([P, 1], F32)
        p = held.tile([P, P], BF16)
        nc.vector.reduce_max(neg_max[:], a[:], axis=X, negate=True)
        nc.scalar.activation(e[:], a[:], EXP, bias=neg_max[:], accum_out=e_sum[:])
        nc.vector.reciprocal(inv_sum[:], e_sum[:])
        nc.vector.tensor_scalar_mul(p[:], e[:], inv_sum[:])

        p_t_psum = psum.tile([P, P], BF16)
        p_t = held.tile([P, P], BF16)
        nc.tensor.transpose(p_t_psum[:], p[:], ident[:])
        fill(1)
        nc.vector.tensor_copy(p_t[:], p_t_psum[:])

        o_t_psum = psum.tile([P, P], F32)
        o_t = held.tile([P, P], BF16)
        nc.tensor.matmul(o_t_psum[:], v_in[:], p_t[:], start=True, stop=True)
        fill(2)
        nc.vector.tensor_copy(o_t[:], o_t_psum[:])

        for m in range(BLOCKS):
            nc.tensor.matmul(
                windows[m][:].indirect(offsets[:]), w_in[:, m * P : (m + 1) * P], o_t[:],
                start=False, stop=True,
            )

        for m in range(BLOCKS):
            for half in (slice(0, S // 2), slice(S // 2, S)):
                z = held.tile([P, S // 2], F32, name=f"z{m}_{half.start}")
                if m % 2 == 0:
                    nc.vector.tensor_copy(z[:], windows[m][:, half])
                else:
                    nc.scalar.copy(z[:], windows[m][:, half])
                nc.sync.dma_start(out[m * P : (m + 1) * P, half], z[:])
